import numpy as np
import ml_dtypes


def mxq(x, axis, fmt="e4m3"):
    dtype, down = {"e4m3": (ml_dtypes.float8_e4m3fn, 7), "e5m2": (ml_dtypes.float8_e5m2, 14)}[fmt]
    v = np.moveaxis(np.asarray(x, np.float32).astype(ml_dtypes.bfloat16).astype(np.float64), axis, -1)
    blocks = v.reshape(v.shape[:-1] + (-1, 32))
    amax = np.abs(blocks).max(-1, keepdims=True)
    byte = np.maximum(np.where(amax > 0, np.frexp(amax)[1] - 1 + 127, 0) - down, 1)
    scale = np.exp2(byte - 127.0)
    codes = (blocks / scale).astype(np.float32).astype(dtype).astype(np.float64)
    return np.moveaxis((codes * scale).reshape(v.shape), -1, axis)


WIDE = False


def mx_kscale(k):
    if not WIDE:
        return np.ones(k)
    levels = np.array([10, -10, 5, -5, 0])
    if k % 512:
        return np.exp2(np.random.permutation(np.resize(levels, k // 32))).repeat(32)
    a = np.empty((k // 512, 16))
    for p in range(k // 512):
        a[p, :8] = np.random.permutation(np.resize(levels, 8))
        for g in range(8):
            far = levels[np.abs(levels - a[p, g]) >= 10]
            a[p, g + 8] = far[np.random.randint(len(far))]
    return np.exp2(a.ravel()).repeat(32)


def f64(x):
    return np.asarray(x).astype(np.float64)


def striped(idx):
    return np.tile(idx.reshape(-1, 16).T, (8, 1)).astype(np.uint16)


def unstriped(offs):
    return offs[:16].T.reshape(-1).astype(np.int64)


E2M1 = np.array([0.0, 0.5, 1.0, 1.5, 2.0, 3.0, 4.0, 6.0, -0.0, -0.5, -1.0, -1.5, -2.0, -3.0, -4.0, -6.0])


def pack_weight(w, fmt):
    k, n = w.shape
    w = f64(np.asarray(w, np.float32).astype(ml_dtypes.bfloat16)).reshape(k // 32, 32, n)
    amax = np.abs(w).max(1)
    if fmt == "e4m3":
        byte = np.frexp(amax)[1] - 1 + 127 - 7
    else:
        mant, ex = np.frexp(amax / 6.0)
        byte = np.where(mant > 0.5, ex, ex - 1) + 127
    byte = np.clip(np.where(amax > 0, byte, 1), 1, 254)
    scaled = (w * np.exp2(127.0 - byte)[:, None, :]).reshape(k, n).astype(np.float32)
    by_word = np.ascontiguousarray(scaled.reshape(k // 512, 128, 4, n).transpose(0, 1, 3, 2))
    if fmt == "e4m3":
        words = by_word.astype(ml_dtypes.float8_e4m3fn).view(np.uint8)
    else:
        c = by_word.astype(ml_dtypes.float4_e2m1fn).view(np.uint8) & 0xF
        words = (c[..., 0::2] | (c[..., 1::2] << 4)).reshape(k // 512, 128, 2 * n)
    return np.ascontiguousarray(words), np.ascontiguousarray(byte.astype(np.uint8).reshape(k // 512, 16, n))


def unpack_weight(words, scales, fmt):
    g, _, n = scales.shape
    words = np.ascontiguousarray(words).reshape(g, 128, n, -1)
    if fmt == "e4m3":
        vals = words.view(ml_dtypes.float8_e4m3fn).astype(np.float64)
    else:
        nib = np.empty((g, 128, n, 4), np.uint8)
        nib[..., 0::2] = words & 0xF
        nib[..., 1::2] = words >> 4
        vals = E2M1[nib]
    vals = vals * np.repeat(np.exp2(scales.astype(np.float64) - 127.0), 8, axis=1)[..., None]
    return vals.transpose(0, 1, 3, 2).reshape(g * 512, n)


def gelu(v):
    return 0.5 * v * (1.0 + np.tanh(np.sqrt(2.0 / np.pi) * (v + 0.044715 * v**3)))


K, H, N, T, S, P, P2 = 512, 512, 768, 4096, 2048, 1024, 512

def setup_inputs():
    n = np.random.standard_normal
    s = mx_kscale(K)[:, None]
    u = mx_kscale(H)[:, None]
    tab_words, tab_scales = pack_weight(n((K, T)) * s, "e4m3")
    w1 = (n((K, H)) / np.sqrt(K) / s * u.T).astype(np.float32)
    w2_words, w2_scales = pack_weight(0.35 * n((K, H)) / np.sqrt(K) / s, "e2m1")
    w3 = (0.7 * n((K, H)) / np.sqrt(K) / s * u.T).astype(np.float32)
    b2 = np.random.uniform(-1.2, 1.2, H).astype(np.float32)
    w4_words, w4_scales = pack_weight(n((H, N)) / np.sqrt(H) / u, "e4m3")
    offs = striped(np.random.permutation(T)[:S])
    pos1 = striped(np.random.permutation(S)[:P])
    pos2 = striped(np.random.permutation(S)[:P])
    pos3 = striped(np.random.permutation(P)[:P2])
    pos4 = striped(np.random.permutation(S)[:P2])
    return {"tab_words": tab_words, "tab_scales": tab_scales, "w1": w1,
            "w2_words": w2_words, "w2_scales": w2_scales, "b2": b2, "w3": w3,
            "w4_words": w4_words, "w4_scales": w4_scales, "offs": offs,
            "pos1": pos1, "pos2": pos2, "pos3": pos3, "pos4": pos4}

def reference(tab_words, tab_scales, w1, w2_words, w2_scales, b2, w3,
              w4_words, w4_scales, offs, pos1, pos2, pos3, pos4):
    v = unpack_weight(tab_words, tab_scales, "e4m3")[:, unstriped(offs)]
    w2 = unpack_weight(w2_words, w2_scales, "e2m1")
    w4 = unpack_weight(w4_words, w4_scales, "e4m3")
    e1 = mxq(f64(w1), 0, "e4m3").T @ v
    e2 = w2.T @ v
    e3 = mxq(f64(w3), 0, "e4m3").T @ v
    h = e1 * np.cos(e2 + f64(b2)[:, None]) + e3
    a1 = np.minimum(h[:, unstriped(pos1)], h[:, unstriped(pos2)])
    a2 = a1[:, unstriped(pos3)] + np.abs(h[:, unstriped(pos4)])
    return w4.T @ mxq(a2, 0, "e4m3")

@@ -1,0 +1,204 @@
+from contextlib import ExitStack
+
+import concourse.mybir as mybir
+
+K, H, N, T, S, PAIRS, KEPT = 512, 512, 768, 4096, 2048, 1024, 512
+FLOPS = 2 * K * H * S * 3 + 2 * H * N * KEPT
+
+F32 = mybir.dt.float32
+BF16 = mybir.dt.bfloat16
+I32 = mybir.dt.int32
+U32 = mybir.dt.uint32
+U16 = mybir.dt.uint16
+U8 = mybir.dt.uint8
+FP8X4 = mybir.dt.float8_e4m3fn_x4
+FP4X4 = mybir.dt.float4_e2m1fn_x4
+ACT = mybir.ActivationFunctionType
+ALU = mybir.AluOpType
+
+P = 128
+PACK = 4
+CHUNK = 512
+OUT_CHUNKS = (256, 256)
+
+
+def load_scale_rows(queue, plane, scales):
+    for quad in range(4):
+        queue.dma_start(
+            out=plane[32 * quad : 32 * quad + 4, :].bitcast(I32),
+            in_=scales[0, 4 * quad : 4 * quad + 4, :].bitcast(I32),
+        )
+
+
+def tile_list_case_link_features_kernel(
+    tc, tab_words, tab_scales, w1, w2_words, w2_scales, b2, w3, w4_words, w4_scales,
+    offs, pos1, pos2, pos3, pos4, out,
+):
+    nc = tc.nc
+    with ExitStack() as ctx:
+        keep = ctx.enter_context(tc.tile_pool(name="keep", bufs=1))
+        ring = ctx.enter_context(tc.tile_pool(name="ring", bufs=3))
+        psum = ctx.enter_context(tc.psum_pool(name="psum", bufs=1))
+
+        offs_sb = keep.tile([P, S // 16], U16, name="offs_sb")
+        pos1_sb = keep.tile([P, PAIRS // 16], U16, name="pos1_sb")
+        pos2_sb = keep.tile([P, PAIRS // 16], U16, name="pos2_sb")
+        pos3_sb = keep.tile([P, KEPT // 16], U16, name="pos3_sb")
+        pos4_sb = keep.tile([P, KEPT // 16], U16, name="pos4_sb")
+
+        tab_plane = keep.tile([P, T], U8, name="tab_plane", align_bytes=64)
+        tab_codes = keep.tile([P, T], U32, name="tab_codes", align_bytes=64)
+        w2_plane_raw = keep.tile([P, H], U8, name="w2_plane_raw", tag="plane_in", align_bytes=64)
+        w2_raw = keep.tile([P, 2 * H], U8, name="w2_raw", tag="codes_in", align_bytes=64)
+        w1_raw = keep.tile([P, PACK, H], F32, name="w1_raw")
+        bias = keep.tile([P, PACK], F32, name="bias")
+
+        plane_words = tab_plane[:].bitcast(I32)
+        nc.vector.memset(plane_words[:, : 5 * T // 32], 0)
+        nc.gpsimd.memset(plane_words[:, 5 * T // 32 :], 0)
+        nc.gpsimd.memset(w2_plane_raw[:].bitcast(I32), 0)
+
+        w3_raw = keep.tile([P, PACK, H], F32, name="w3_raw")
+        nc.sync.dma_start(offs_sb[:], offs)
+        load_scale_rows(nc.sync, tab_plane, tab_scales)
+        nc.sync.dma_start(pos1_sb[:], pos1)
+        nc.sync.dma_start(pos2_sb[:], pos2)
+        nc.sync.dma_start(pos4_sb[:], pos4)
+        nc.sync.dma_start(
+            out=tab_codes[:].bitcast(I32), in_=tab_words[0].rearrange("p t i -> p (t i)").bitcast(I32)
+        )
+        nc.sync.dma_start(out=w1_raw[:], in_=w1.rearrange("(p j) r -> p j r", j=PACK))
+        load_scale_rows(nc.sync, w2_plane_raw, w2_scales)
+        nc.sync.dma_start(out=w2_raw[:].bitcast(I32), in_=w2_words[0].bitcast(I32))
+        nc.sync.dma_start(out=bias[:], in_=b2.rearrange("(p t) -> p t", t=PACK))
+        nc.sync.dma_start(out=w3_raw[:], in_=w3.rearrange("(p j) r -> p j r", j=PACK))
+        nc.sync.dma_start(pos3_sb[:], pos3)
+
+        def quantise_weight(raw, copy, name):
+            grouped = keep.tile([P, PACK * H], BF16, name=name + "_grouped", align_bytes=64)
+            codes = keep.tile([P, H], U32, name=name + "_codes", align_bytes=64)
+            plane = keep.tile([P, H], U8, name=name + "_plane", align_bytes=64)
+            copy(
+                out=grouped[:].rearrange("p (t m j) -> p m j t", t=PACK, j=PACK),
+                in_=raw[:].rearrange("p j (m t) -> p m j t", t=PACK),
+            )
+            nc.vector.quantize_mx(out=codes[:].bitcast(FP8X4), scales=plane[:], in_=grouped[:])
+            return codes, plane
+
+        v_plane = keep.tile([P, S], U8, name="v_plane", align_bytes=64)
+        nc.vector.tensor_copy(v_plane[:], tab_plane[:].indirect(offs_sb[:]))
+        v_codes = []
+        for c in range(S // CHUNK):
+            picked = keep.tile([P, CHUNK], U32, name="v_codes%d" % c, align_bytes=64)
+            cols = slice(c * CHUNK // 16, (c + 1) * CHUNK // 16)
+            nc.vector.tensor_copy(picked[:], tab_codes[:].indirect(offs_sb[:, cols]))
+            v_codes.append(picked)
+
+        w2_codes = keep.tile([P, 2 * H], U8, name="w2_codes", align_bytes=64)
+        w2_plane = keep.tile([P, H], U8, name="w2_plane", align_bytes=64)
+        nc.scalar.copy(
+            out=w2_codes[:].bitcast(U16).rearrange("p (t m) -> p m t", t=PACK),
+            in_=w2_raw[:].bitcast(U16).rearrange("p (m t) -> p m t", t=PACK),
+        )
+        nc.gpsimd.tensor_copy(
+            out=w2_plane[:].rearrange("p (t m) -> p t m", t=PACK),
+            in_=w2_plane_raw[:].rearrange("p (m t) -> p t m", t=PACK),
+        )
+        half_bias = keep.tile([P, PACK], F32, name="half_bias")
+        nc.gpsimd.tensor_scalar(half_bias[:], bias[:], 0.5, 0.0, ALU.mult, ALU.add)
+        w1_codes, w1_plane = quantise_weight(w1_raw, nc.scalar.copy, "w1")
+        w3_codes, w3_plane = quantise_weight(w3_raw, nc.vector.tensor_copy, "w3")
+
+        w4_codes = keep.tile([P, N], U32, name="w4_codes", tag="codes_in", align_bytes=64)
+        w4_plane = keep.tile([P, N], U8, name="w4_plane", tag="plane_in", align_bytes=64)
+        nc.gpsimd.memset(w4_plane[:].bitcast(I32), 0)
+        nc.sync.dma_start(
+            out=w4_codes[:].bitcast(I32),
+            in_=w4_words[0].rearrange("p c i -> p (c i)").bitcast(I32),
+        )
+        load_scale_rows(nc.sync, w4_plane, w4_scales)
+
+        pair_min = []
+        recent_abs = []
+        for t in range(PACK):
+            rows = slice(t * P, (t + 1) * P)
+            h = keep.tile([P, S], F32, name="h%d" % t)
+            for c in range(S // CHUNK):
+                cols = slice(c * CHUNK, (c + 1) * CHUNK)
+                moving = v_codes[c][:].bitcast(FP8X4)
+                e2 = psum.tile([P, CHUNK], F32, name="e2", tag="e2", bufs=2)
+                e1 = psum.tile([P, CHUNK], F32, name="e1", tag="e1", bufs=3)
+                e3 = psum.tile([P, CHUNK], F32, name="e3", tag="e3", bufs=3)
+                nc.tensor.matmul_mx(
+                    out=e2[:], lhsT=w2_codes[:, 2 * t * P : 2 * (t + 1) * P].bitcast(FP4X4),
+                    lhsT_scale=w2_plane[:, rows], rhs=moving, rhs_scale=v_plane[:, cols],
+                    start=True, stop=True,
+                )
+                nc.tensor.matmul_mx(
+                    out=e1[:], lhsT=w1_codes[:, rows].bitcast(FP8X4), lhsT_scale=w1_plane[:, rows],
+                    rhs=moving, rhs_scale=v_plane[:, cols], start=True, stop=True,
+                )
+                nc.tensor.matmul_mx(
+                    out=e3[:], lhsT=w3_codes[:, rows].bitcast(FP8X4), lhsT_scale=w3_plane[:, rows],
+                    rhs=moving, rhs_scale=v_plane[:, cols], start=True, stop=True,
+                )
+                sine = ring.tile([P, CHUNK], F32, name="sine")
+                nc.scalar.activation(sine[:], e2[:], ACT.Sin, bias=half_bias[:, t : t + 1], scale=0.5)
+                sine2 = ring.tile([P, CHUNK], F32, name="sine2")
+                nc.scalar.activation(sine2[:], sine[:], ACT.Square)
+                prod = ring.tile([P, CHUNK], F32, name="prod")
+                nc.vector.scalar_tensor_tensor(prod[:], sine2[:], 0.5, e1[:], ALU.subtract, ALU.mult)
+                nc.vector.scalar_tensor_tensor(h[:, cols], prod[:], -2.0, e3[:], ALU.mult, ALU.add)
+
+            first = ring.tile([P, PAIRS], F32, name="first", bufs=2)
+            second = ring.tile([P, PAIRS], F32, name="second", bufs=2)
+            recent = ring.tile([P, KEPT], F32, name="recent", bufs=2)
+            nc.vector.tensor_copy(first[:], h[:].indirect(pos1_sb[:]))
+            nc.vector.tensor_copy(second[:], h[:].indirect(pos2_sb[:]))
+            nc.vector.tensor_copy(recent[:], h[:].indirect(pos4_sb[:]))
+            a1 = keep.tile([P, PAIRS], F32, name="a1_%d" % t)
+            nc.vector.tensor_tensor(a1[:], first[:], second[:], ALU.min)
+            size = keep.tile([P, KEPT], F32, name="size%d" % t)
+            nc.scalar.activation(size[:], recent[:], ACT.Abs)
+            pair_min.append(a1)
+            recent_abs.append(size)
+
+        m0 = 0
+        out_rows = out.rearrange("(a p) m -> p a m", p=P)
+        for i, width in enumerate(OUT_CHUNKS):
+            last = i == len(OUT_CHUNKS) - 1
+            cols = slice(m0, m0 + width)
+            a2 = keep.tile([P, PACK, width], F32, name="a2_%d" % i)
+            for t in range(PACK):
+                nc.vector.tensor_tensor(
+                    a2[:, t, :],
+                    pair_min[t][:].indirect(pos3_sb[:, m0 // 16 : (m0 + width) // 16]),
+                    recent_abs[t][:, cols],
+                    ALU.add,
+                )
+            grouped = keep.tile([P, PACK * width], BF16, name="a2_grouped%d" % i, align_bytes=64)
+            copy = nc.vector.tensor_copy if last else nc.scalar.copy
+            copy(
+                out=grouped[:].rearrange("p (c i t) -> p c t i", i=4, t=PACK),
+                in_=a2[:].rearrange("p t (c i) -> p c t i", i=4),
+            )
+            codes = keep.tile([P, width], U32, name="a2_codes%d" % i, align_bytes=64)
+            plane = keep.tile([P, width], U8, name="a2_plane%d" % i, align_bytes=64)
+            nc.vector.quantize_mx(out=codes[:].bitcast(FP8X4), scales=plane[:], in_=grouped[:])
+            per_bank = CHUNK // width
+            for b in range(N // P // per_bank):
+                acc = psum.tile([P, per_bank, width], F32, name="acc", tag="e1" if i % 2 == 0 else "e3", bufs=3)
+                for a in range(per_bank):
+                    n_cols = slice((b * per_bank + a) * P, (b * per_bank + a + 1) * P)
+                    nc.tensor.matmul_mx(
+                        out=acc[:, a, :], lhsT=w4_codes[:, n_cols].bitcast(FP8X4),
+                        lhsT_scale=w4_plane[:, n_cols], rhs=codes[:].bitcast(FP8X4),
+                        rhs_scale=plane[:], start=True, stop=True,
+                    )
+                staged = keep.tile([P, per_bank, width], F32, name="staged%d_%d" % (i, b))
+                drain = nc.vector.tensor_copy if last and b % 2 == 1 else nc.scalar.copy
+                drain(out=staged[:], in_=acc[:])
+                nc.sync.dma_start(
+                    out=out_rows[:, b * per_bank : (b + 1) * per_bank, cols], in_=staged[:]
+                )
+            m0 = m0 + width

@@ -1,5 +1,7 @@
 from contextlib import ExitStack
 
+import math
+
 import concourse.mybir as mybir
 
 K, H, N, T, S, PAIRS, KEPT = 512, 512, 768, 4096, 2048, 1024, 512
@@ -19,7 +21,7 @@ ALU = mybir.AluOpType
 P = 128
 PACK = 4
 CHUNK = 512
-OUT_CHUNKS = (256, 256)
+OUT_CHUNKS = (256, 128, 128)
 
 
 def load_scale_rows(queue, plane, scales):
@@ -61,17 +63,17 @@ def tile_list_case_link_features_kernel(
         w3_raw = keep.tile([P, PACK, H], F32, name="w3_raw")
         nc.sync.dma_start(offs_sb[:], offs)
         load_scale_rows(nc.sync, tab_plane, tab_scales)
-        nc.sync.dma_start(pos1_sb[:], pos1)
-        nc.sync.dma_start(pos2_sb[:], pos2)
-        nc.sync.dma_start(pos4_sb[:], pos4)
+        nc.sync.dma_start(out=w2_raw[:].bitcast(I32), in_=w2_words[0].bitcast(I32))
+        nc.sync.dma_start(out=bias[:], in_=b2.rearrange("(p t) -> p t", t=PACK))
         nc.sync.dma_start(
             out=tab_codes[:].bitcast(I32), in_=tab_words[0].rearrange("p t i -> p (t i)").bitcast(I32)
         )
-        nc.sync.dma_start(out=w1_raw[:], in_=w1.rearrange("(p j) r -> p j r", j=PACK))
         load_scale_rows(nc.sync, w2_plane_raw, w2_scales)
-        nc.sync.dma_start(out=w2_raw[:].bitcast(I32), in_=w2_words[0].bitcast(I32))
-        nc.sync.dma_start(out=bias[:], in_=b2.rearrange("(p t) -> p t", t=PACK))
+        nc.sync.dma_start(out=w1_raw[:], in_=w1.rearrange("(p j) r -> p j r", j=PACK))
         nc.sync.dma_start(out=w3_raw[:], in_=w3.rearrange("(p j) r -> p j r", j=PACK))
+        nc.sync.dma_start(pos1_sb[:], pos1)
+        nc.sync.dma_start(pos2_sb[:], pos2)
+        nc.sync.dma_start(pos4_sb[:], pos4)
         nc.sync.dma_start(pos3_sb[:], pos3)
 
         def quantise_weight(raw, copy, name):
@@ -79,8 +81,8 @@ def tile_list_case_link_features_kernel(
             codes = keep.tile([P, H], U32, name=name + "_codes", align_bytes=64)
             plane = keep.tile([P, H], U8, name=name + "_plane", align_bytes=64)
             copy(
-                out=grouped[:].rearrange("p (t m j) -> p m j t", t=PACK, j=PACK),
-                in_=raw[:].rearrange("p j (m t) -> p m j t", t=PACK),
+                out=grouped[:].rearrange("p (t m j) -> p m t j", t=PACK, j=PACK),
+                in_=raw[:].rearrange("p j (m t) -> p m t j", t=PACK),
             )
             nc.vector.quantize_mx(out=codes[:].bitcast(FP8X4), scales=plane[:], in_=grouped[:])
             return codes, plane
@@ -118,74 +120,105 @@ def tile_list_case_link_features_kernel(
         )
         load_scale_rows(nc.sync, w4_plane, w4_scales)
 
-        pair_min = []
-        recent_abs = []
-        for t in range(PACK):
+        def products(t, c):
             rows = slice(t * P, (t + 1) * P)
-            h = keep.tile([P, S], F32, name="h%d" % t)
-            for c in range(S // CHUNK):
-                cols = slice(c * CHUNK, (c + 1) * CHUNK)
-                moving = v_codes[c][:].bitcast(FP8X4)
-                e2 = psum.tile([P, CHUNK], F32, name="e2", tag="e2", bufs=2)
-                e1 = psum.tile([P, CHUNK], F32, name="e1", tag="e1", bufs=3)
-                e3 = psum.tile([P, CHUNK], F32, name="e3", tag="e3", bufs=3)
+            cols = slice(c * CHUNK, (c + 1) * CHUNK)
+            moving = v_codes[c][:].bitcast(FP8X4)
+            e2 = psum.tile([P, CHUNK], F32, name="e2", tag="e2", bufs=2)
+            e1 = psum.tile([P, CHUNK], F32, name="e1", tag="e1", bufs=3)
+            e3 = psum.tile([P, CHUNK], F32, name="e3", tag="e3", bufs=3)
+            for acc, codes, plane in (
+                (e2, w2_codes[:, 2 * t * P : 2 * (t + 1) * P].bitcast(FP4X4), w2_plane),
+                (e3, w3_codes[:, rows].bitcast(FP8X4), w3_plane),
+                (e1, w1_codes[:, rows].bitcast(FP8X4), w1_plane),
+            ):
                 nc.tensor.matmul_mx(
-                    out=e2[:], lhsT=w2_codes[:, 2 * t * P : 2 * (t + 1) * P].bitcast(FP4X4),
-                    lhsT_scale=w2_plane[:, rows], rhs=moving, rhs_scale=v_plane[:, cols],
-                    start=True, stop=True,
+                    out=acc[:], lhsT=codes, lhsT_scale=plane[:, rows], rhs=moving,
+                    rhs_scale=v_plane[:, cols], start=True, stop=True,
                 )
-                nc.tensor.matmul_mx(
-                    out=e1[:], lhsT=w1_codes[:, rows].bitcast(FP8X4), lhsT_scale=w1_plane[:, rows],
-                    rhs=moving, rhs_scale=v_plane[:, cols], start=True, stop=True,
-                )
-                nc.tensor.matmul_mx(
-                    out=e3[:], lhsT=w3_codes[:, rows].bitcast(FP8X4), lhsT_scale=w3_plane[:, rows],
-                    rhs=moving, rhs_scale=v_plane[:, cols], start=True, stop=True,
-                )
-                sine = ring.tile([P, CHUNK], F32, name="sine")
-                nc.scalar.activation(sine[:], e2[:], ACT.Sin, bias=half_bias[:, t : t + 1], scale=0.5)
-                sine2 = ring.tile([P, CHUNK], F32, name="sine2")
-                nc.scalar.activation(sine2[:], sine[:], ACT.Square)
-                prod = ring.tile([P, CHUNK], F32, name="prod")
-                nc.vector.scalar_tensor_tensor(prod[:], sine2[:], 0.5, e1[:], ALU.subtract, ALU.mult)
-                nc.vector.scalar_tensor_tensor(h[:, cols], prod[:], -2.0, e3[:], ALU.mult, ALU.add)
+            return e1, e2, e3
 
-            first = ring.tile([P, PAIRS], F32, name="first", bufs=2)
-            second = ring.tile([P, PAIRS], F32, name="second", bufs=2)
-            recent = ring.tile([P, KEPT], F32, name="recent", bufs=2)
-            nc.vector.tensor_copy(first[:], h[:].indirect(pos1_sb[:]))
-            nc.vector.tensor_copy(second[:], h[:].indirect(pos2_sb[:]))
-            nc.vector.tensor_copy(recent[:], h[:].indirect(pos4_sb[:]))
-            a1 = keep.tile([P, PAIRS], F32, name="a1_%d" % t)
+        def minus_cos_times(t, e1, e2, sine, square, prod):
+            nc.scalar.activation(sine[:], e2[:], ACT.Sin, bias=half_bias[:, t : t + 1], scale=0.5)
+            nc.scalar.activation(square, sine[:], ACT.Square, scale=math.sqrt(2.0))
+            nc.vector.scalar_tensor_tensor(prod, square, 1.0, e1[:], ALU.subtract, ALU.mult)
+
+        h = [keep.tile([P, S], F32, name="h%d" % t) for t in range(PACK)]
+        for c in range(S // CHUNK):
+            e1, e2, e3 = products(0, c)
+            square = ring.tile([P, CHUNK], F32, name="square")
+            prod = ring.tile([P, CHUNK], F32, name="prod")
+            sine = ring.tile([P, CHUNK], F32, name="sine", bufs=2)
+            minus_cos_times(0, e1, e2, sine, square[:], prod[:])
+            nc.vector.tensor_tensor(h[0][:, c * CHUNK : (c + 1) * CHUNK], e3[:], prod[:], ALU.subtract)
+
+        low, high = slice(0, CHUNK), slice(CHUNK, 2 * CHUNK)
+        low16, high16 = slice(0, CHUNK // 16), slice(CHUNK // 16, 2 * CHUNK // 16)
+        pair_min = []
+        recents = []
+        for t in range(PACK):
+            first = ring.tile([P, PAIRS], F32, name="first", tag="first", bufs=2)
+            second = ring.tile([P, PAIRS], F32, name="second", tag="second", bufs=2)
+            recent = keep.tile([P, KEPT], F32, name="recent%d" % t)
+            picks = (
+                (first[:, low], pos1_sb[:, low16]),
+                (first[:, high], pos1_sb[:, high16]),
+                (second[:, low], pos2_sb[:, low16]),
+                (second[:, high], pos2_sb[:, high16]),
+            )
+            if t + 1 < PACK:
+                used_terms = []
+            for c, (place, offsets) in enumerate(picks):
+                if t + 1 < PACK:
+                    e1, e2, e3 = products(t + 1, c)
+                    if c + 1 < len(picks):
+                        terms = ring.tile([P, 2 * CHUNK], F32, name="terms")
+                        sine = ring.tile([P, CHUNK], F32, name="sine", bufs=2)
+                    else:
+                        terms = keep.tile([P, 2 * CHUNK], F32, name="terms%d" % t, tag="a1_%d" % t)
+                        sine = recent
+                    minus_cos_times(t + 1, e1, e2, sine, place, terms[:, low])
+                    nc.scalar.copy(terms[:, high], e3[:])
+                    nc.gpsimd.tensor_tensor(
+                        h[t + 1][:, c * CHUNK : (c + 1) * CHUNK], terms[:, high], terms[:, low], ALU.subtract
+                    )
+                    used_terms.append(terms)
+                nc.vector.tensor_copy(place, h[t][:].indirect(offsets))
+            nc.vector.tensor_copy(recent[:], h[t][:].indirect(pos4_sb[:]))
+            a1 = keep.tile([P, PAIRS], F32, name="a1_%d" % t, tag="a1_%d" % t)
             nc.vector.tensor_tensor(a1[:], first[:], second[:], ALU.min)
-            size = keep.tile([P, KEPT], F32, name="size%d" % t)
-            nc.scalar.activation(size[:], recent[:], ACT.Abs)
             pair_min.append(a1)
-            recent_abs.append(size)
+            recents.append(recent)
 
+        last_size = keep.tile([P, KEPT], F32, name="last_size")
+        sizes = [terms[:, low] for terms in used_terms[: PACK - 1]] + [last_size[:]]
+        for t in range(PACK):
+            nc.scalar.activation(sizes[t], recents[t][:], ACT.Abs)
+
+        sum_places = (first[:], second[:, low], second[:, high])
         m0 = 0
         out_rows = out.rearrange("(a p) m -> p a m", p=P)
         for i, width in enumerate(OUT_CHUNKS):
             last = i == len(OUT_CHUNKS) - 1
             cols = slice(m0, m0 + width)
-            a2 = keep.tile([P, PACK, width], F32, name="a2_%d" % i)
+            a2 = sum_places[i].rearrange("p (t m) -> p t m", t=PACK)
             for t in range(PACK):
                 nc.vector.tensor_tensor(
                     a2[:, t, :],
                     pair_min[t][:].indirect(pos3_sb[:, m0 // 16 : (m0 + width) // 16]),
-                    recent_abs[t][:, cols],
+                    sizes[t][:, cols],
                     ALU.add,
                 )
             grouped = keep.tile([P, PACK * width], BF16, name="a2_grouped%d" % i, align_bytes=64)
             copy = nc.vector.tensor_copy if last else nc.scalar.copy
             copy(
                 out=grouped[:].rearrange("p (c i t) -> p c t i", i=4, t=PACK),
-                in_=a2[:].rearrange("p t (c i) -> p c t i", i=4),
+                in_=a2.rearrange("p t (c i) -> p c t i", i=4),
             )
             codes = keep.tile([P, width], U32, name="a2_codes%d" % i, align_bytes=64)
             plane = keep.tile([P, width], U8, name="a2_plane%d" % i, align_bytes=64)
             nc.vector.quantize_mx(out=codes[:].bitcast(FP8X4), scales=plane[:], in_=grouped[:])
-            per_bank = CHUNK // width
+            per_bank = 2 if width == 256 else 3
             for b in range(N // P // per_bank):
                 acc = psum.tile([P, per_bank, width], F32, name="acc", tag="e1" if i % 2 == 0 else "e3", bufs=3)
                 for a in range(per_bank):

@@ -25,10 +25,10 @@ OUT_CHUNKS = (256, 128, 128)
 
 
 def load_scale_rows(queue, plane, scales):
-    for quad in range(4):
+    for row in range(4):
         queue.dma_start(
-            out=plane[32 * quad : 32 * quad + 4, :].bitcast(I32),
-            in_=scales[0, 4 * quad : 4 * quad + 4, :].bitcast(I32),
+            out=plane[row:P:32, :].bitcast(I32),
+            in_=scales[0, row:16:4, :].bitcast(I32),
         )
 
 
@@ -76,14 +76,14 @@ def tile_list_case_link_features_kernel(
         nc.sync.dma_start(pos4_sb[:], pos4)
         nc.sync.dma_start(pos3_sb[:], pos3)
 
-        def quantise_weight(raw, copy, name):
+        def quantise_weight(raw, shares, name):
             grouped = keep.tile([P, PACK * H], BF16, name=name + "_grouped", align_bytes=64)
             codes = keep.tile([P, H], U32, name=name + "_codes", align_bytes=64)
             plane = keep.tile([P, H], U8, name=name + "_plane", align_bytes=64)
-            copy(
-                out=grouped[:].rearrange("p (t m j) -> p m t j", t=PACK, j=PACK),
-                in_=raw[:].rearrange("p j (m t) -> p m t j", t=PACK),
-            )
+            dealt = grouped[:].rearrange("p (t m j) -> p m t j", t=PACK, j=PACK)
+            source = raw[:].rearrange("p j (m t) -> p m t j", t=PACK)
+            for copy, part, walk in shares:
+                copy(out=dealt[:, part].rearrange(walk), in_=source[:, part].rearrange(walk))
             nc.vector.quantize_mx(out=codes[:].bitcast(FP8X4), scales=plane[:], in_=grouped[:])
             return codes, plane
 
@@ -99,8 +99,8 @@ def tile_list_case_link_features_kernel(
         w2_codes = keep.tile([P, 2 * H], U8, name="w2_codes", align_bytes=64)
         w2_plane = keep.tile([P, H], U8, name="w2_plane", align_bytes=64)
         nc.scalar.copy(
-            out=w2_codes[:].bitcast(U16).rearrange("p (t m) -> p m t", t=PACK),
-            in_=w2_raw[:].bitcast(U16).rearrange("p (m t) -> p m t", t=PACK),
+            out=w2_codes[:].bitcast(U16).rearrange("p (t m) -> p t m", t=PACK),
+            in_=w2_raw[:].bitcast(U16).rearrange("p (m t) -> p t m", t=PACK),
         )
         nc.gpsimd.tensor_copy(
             out=w2_plane[:].rearrange("p (t m) -> p t m", t=PACK),
@@ -108,8 +108,17 @@ def tile_list_case_link_features_kernel(
         )
         half_bias = keep.tile([P, PACK], F32, name="half_bias")
         nc.gpsimd.tensor_scalar(half_bias[:], bias[:], 0.5, 0.0, ALU.mult, ALU.add)
-        w1_codes, w1_plane = quantise_weight(w1_raw, nc.scalar.copy, "w1")
-        w3_codes, w3_plane = quantise_weight(w3_raw, nc.vector.tensor_copy, "w3")
+        one = keep.tile([P, 1], F32, name="one")
+        half_pi = keep.tile([P, 1], F32, name="half_pi")
+        nc.gpsimd.memset(one[:], 1.0)
+        nc.gpsimd.tensor_scalar(half_pi[:], one[:], math.pi / 2, 0.0, ALU.mult, ALU.add)
+        w1_codes, w1_plane = quantise_weight(
+            w1_raw, (
+                (nc.scalar.copy, slice(0, 80), "p m t j -> p m t j"),
+                (nc.gpsimd.tensor_copy, slice(80, P), "p m t j -> p t m j"),
+            ), "w1"
+        )
+        w3_codes, w3_plane = quantise_weight(w3_raw, ((nc.vector.tensor_copy, slice(0, P), "p m t j -> p m t j"),), "w3")
 
         w4_codes = keep.tile([P, N], U32, name="w4_codes", tag="codes_in", align_bytes=64)
         w4_plane = keep.tile([P, N], U8, name="w4_plane", tag="plane_in", align_bytes=64)
@@ -138,26 +147,31 @@ def tile_list_case_link_features_kernel(
                 )
             return e1, e2, e3
 
+        def cosine(t, e2, size, cos):
+            nc.scalar.activation(size, e2[:], ACT.Abs, bias=bias[:, t : t + 1])
+            nc.scalar.activation(cos, size, ACT.Sin, bias=half_pi[:], scale=-1.0)
+
         def minus_cos_times(t, e1, e2, sine, square, prod):
-            nc.scalar.activation(sine[:], e2[:], ACT.Sin, bias=half_bias[:, t : t + 1], scale=0.5)
-            nc.scalar.activation(square, sine[:], ACT.Square, scale=math.sqrt(2.0))
+            nc.scalar.activation(sine, e2[:], ACT.Sin, bias=half_bias[:, t : t + 1], scale=0.5)
+            nc.scalar.activation(square, sine, ACT.Square, scale=math.sqrt(2.0))
             nc.vector.scalar_tensor_tensor(prod, square, 1.0, e1[:], ALU.subtract, ALU.mult)
 
         h = [keep.tile([P, S], F32, name="h%d" % t) for t in range(PACK)]
+        first_angle = keep.tile([P, CHUNK], F32, name="first_angle")
         for c in range(S // CHUNK):
             e1, e2, e3 = products(0, c)
-            square = ring.tile([P, CHUNK], F32, name="square")
+            cos = ring.tile([P, CHUNK], F32, name="cos", bufs=4)
             prod = ring.tile([P, CHUNK], F32, name="prod")
-            sine = ring.tile([P, CHUNK], F32, name="sine", bufs=2)
-            minus_cos_times(0, e1, e2, sine, square[:], prod[:])
+            minus_cos_times(0, e1, e2, first_angle[:] if c == 0 else w1_raw[:, c, :], cos[:], prod[:])
             nc.vector.tensor_tensor(h[0][:, c * CHUNK : (c + 1) * CHUNK], e3[:], prod[:], ALU.subtract)
 
         low, high = slice(0, CHUNK), slice(CHUNK, 2 * CHUNK)
         low16, high16 = slice(0, CHUNK // 16), slice(CHUNK // 16, 2 * CHUNK // 16)
         pair_min = []
         recents = []
+        spent = keep.tile([P, PAIRS], F32, name="spent")
         for t in range(PACK):
-            first = ring.tile([P, PAIRS], F32, name="first", tag="first", bufs=2)
+            first = ring.tile([P, PAIRS], F32, name="first", tag="first", bufs=3)
             second = ring.tile([P, PAIRS], F32, name="second", tag="second", bufs=2)
             recent = keep.tile([P, KEPT], F32, name="recent%d" % t)
             picks = (
@@ -173,14 +187,23 @@ def tile_list_case_link_features_kernel(
                     e1, e2, e3 = products(t + 1, c)
                     if c + 1 < len(picks):
                         terms = ring.tile([P, 2 * CHUNK], F32, name="terms")
-                        sine = ring.tile([P, CHUNK], F32, name="sine", bufs=2)
+                        angle = ring.tile([P, CHUNK], F32, name="angle", bufs=2)
                     else:
                         terms = keep.tile([P, 2 * CHUNK], F32, name="terms%d" % t, tag="a1_%d" % t)
-                        sine = recent
-                    minus_cos_times(t + 1, e1, e2, sine, place, terms[:, low])
+                        angle = recent
+                    if c == 0:
+                        cos = ring.tile([P, CHUNK], F32, name="cos", bufs=4)
+                        prod = spent[:, low]
+                        cosine(t + 1, e2, angle[:], cos[:])
+                        nc.scalar.copy(terms[:, low], e1[:])
+                        nc.gpsimd.tensor_tensor(prod, terms[:, low], cos[:], ALU.mult)
+                    else:
+                        prod = terms[:, low]
+                        minus_cos_times(t + 1, e1, e2, angle[:], place, prod)
                     nc.scalar.copy(terms[:, high], e3[:])
                     nc.gpsimd.tensor_tensor(
-                        h[t + 1][:, c * CHUNK : (c + 1) * CHUNK], terms[:, high], terms[:, low], ALU.subtract
+                        h[t + 1][:, c * CHUNK : (c + 1) * CHUNK], terms[:, high], prod,
+                        ALU.add if c == 0 else ALU.subtract,
                     )
                     used_terms.append(terms)
                 nc.vector.tensor_copy(place, h[t][:].indirect(offsets))
@@ -189,19 +212,23 @@ def tile_list_case_link_features_kernel(
             nc.vector.tensor_tensor(a1[:], first[:], second[:], ALU.min)
             pair_min.append(a1)
             recents.append(recent)
+            spent = first
 
         last_size = keep.tile([P, KEPT], F32, name="last_size")
         sizes = [terms[:, low] for terms in used_terms[: PACK - 1]] + [last_size[:]]
         for t in range(PACK):
             nc.scalar.activation(sizes[t], recents[t][:], ACT.Abs)
 
-        sum_places = (first[:], second[:, low], second[:, high])
         m0 = 0
         out_rows = out.rearrange("(a p) m -> p a m", p=P)
         for i, width in enumerate(OUT_CHUNKS):
             last = i == len(OUT_CHUNKS) - 1
             cols = slice(m0, m0 + width)
-            a2 = sum_places[i].rearrange("p (t m) -> p t m", t=PACK)
+            if last:
+                place = keep.tile([P, PACK * width], F32, name="last_sums", tag="a2_grouped0", align_bytes=64)[:]
+            else:
+                place = (first[:], second[:, low])[i]
+            a2 = place.rearrange("p (t m) -> p t m", t=PACK)
             for t in range(PACK):
                 nc.vector.tensor_tensor(
                     a2[:, t, :],
@@ -209,7 +236,7 @@ def tile_list_case_link_features_kernel(
                     sizes[t][:, cols],
                     ALU.add,
                 )
-            grouped = keep.tile([P, PACK * width], BF16, name="a2_grouped%d" % i, align_bytes=64)
+            grouped = keep.tile([P, PACK * width], BF16, name="a2_grouped%d" % i, tag="a2_grouped%d" % i, align_bytes=64)
             copy = nc.vector.tensor_copy if last else nc.scalar.copy
             copy(
                 out=grouped[:].rearrange("p (c i t) -> p c t i", i=4, t=PACK),

@@ -60,7 +60,7 @@ def tile_list_case_link_features_kernel(
         nc.gpsimd.memset(plane_words[:, 5 * T // 32 :], 0)
         nc.gpsimd.memset(w2_plane_raw[:].bitcast(I32), 0)
 
-        w3_raw = keep.tile([P, PACK, H], F32, name="w3_raw")
+        w3_raw = keep.tile([P, PACK, H], F32, name="w3_raw", tag="w3_raw", align_bytes=64)
         nc.sync.dma_start(offs_sb[:], offs)
         load_scale_rows(nc.sync, tab_plane, tab_scales)
         nc.sync.dma_start(out=w2_raw[:].bitcast(I32), in_=w2_words[0].bitcast(I32))
@@ -76,14 +76,18 @@ def tile_list_case_link_features_kernel(
         nc.sync.dma_start(pos4_sb[:], pos4)
         nc.sync.dma_start(pos3_sb[:], pos3)
 
-        def quantise_weight(raw, shares, name):
-            grouped = keep.tile([P, PACK * H], BF16, name=name + "_grouped", align_bytes=64)
-            codes = keep.tile([P, H], U32, name=name + "_codes", align_bytes=64)
-            plane = keep.tile([P, H], U8, name=name + "_plane", align_bytes=64)
+        def deal_weight(raw, shares, name):
+            grouped = keep.tile([P, PACK * H], BF16, name=name, align_bytes=64)
             dealt = grouped[:].rearrange("p (t m j) -> p m t j", t=PACK, j=PACK)
             source = raw[:].rearrange("p j (m t) -> p m t j", t=PACK)
             for copy, part, walk in shares:
                 copy(out=dealt[:, part].rearrange(walk), in_=source[:, part].rearrange(walk))
+            return grouped
+
+        def quantise(grouped, name, codes_tag):
+            width = grouped.shape[1] // PACK
+            codes = keep.tile([P, width], U32, name=name + "_codes", tag=codes_tag, align_bytes=64)
+            plane = keep.tile([P, width], U8, name=name + "_plane", align_bytes=64)
             nc.vector.quantize_mx(out=codes[:].bitcast(FP8X4), scales=plane[:], in_=grouped[:])
             return codes, plane
 
@@ -112,13 +116,19 @@ def tile_list_case_link_features_kernel(
         half_pi = keep.tile([P, 1], F32, name="half_pi")
         nc.gpsimd.memset(one[:], 1.0)
         nc.gpsimd.tensor_scalar(half_pi[:], one[:], math.pi / 2, 0.0, ALU.mult, ALU.add)
-        w1_codes, w1_plane = quantise_weight(
-            w1_raw, (
-                (nc.scalar.copy, slice(0, 80), "p m t j -> p m t j"),
-                (nc.gpsimd.tensor_copy, slice(80, P), "p m t j -> p t m j"),
-            ), "w1"
+        w1_grouped = deal_weight(
+            w1_raw,
+            (
+                (nc.scalar.copy, slice(0, 40), "p m t j -> p m t j"),
+                (nc.gpsimd.tensor_copy, slice(40, P), "p m t j -> p t m j"),
+            ),
+            "w1_grouped",
         )
-        w3_codes, w3_plane = quantise_weight(w3_raw, ((nc.vector.tensor_copy, slice(0, P), "p m t j -> p m t j"),), "w3")
+        w3_grouped = deal_weight(
+            w3_raw, ((nc.vector.tensor_copy, slice(0, P), "p m t j -> p m t j"),), "w3_grouped"
+        )
+        w1_codes, w1_plane = quantise(w1_grouped, "w1", "w3_raw")
+        w3_codes, w3_plane = quantise(w3_grouped, "w3", "w3_codes")
 
         w4_codes = keep.tile([P, N], U32, name="w4_codes", tag="codes_in", align_bytes=64)
         w4_plane = keep.tile([P, N], U8, name="w4_plane", tag="plane_in", align_bytes=64)
@@ -157,16 +167,15 @@ def tile_list_case_link_features_kernel(
             nc.vector.scalar_tensor_tensor(prod, square, 1.0, e1[:], ALU.subtract, ALU.mult)
 
         h = [keep.tile([P, S], F32, name="h%d" % t) for t in range(PACK)]
-        first_angle = keep.tile([P, CHUNK], F32, name="first_angle")
         for c in range(S // CHUNK):
             e1, e2, e3 = products(0, c)
-            cos = ring.tile([P, CHUNK], F32, name="cos", bufs=4)
+            spare = ring.tile([P, CHUNK], F32, name="cos", bufs=4)
             prod = ring.tile([P, CHUNK], F32, name="prod")
-            minus_cos_times(0, e1, e2, first_angle[:] if c == 0 else w1_raw[:, c, :], cos[:], prod[:])
+            sine, square = (spare[:], w1_raw[:, c, :]) if c == 0 else (w1_raw[:, c, :], spare[:])
+            minus_cos_times(0, e1, e2, sine, square, prod[:])
             nc.vector.tensor_tensor(h[0][:, c * CHUNK : (c + 1) * CHUNK], e3[:], prod[:], ALU.subtract)
 
         low, high = slice(0, CHUNK), slice(CHUNK, 2 * CHUNK)
-        low16, high16 = slice(0, CHUNK // 16), slice(CHUNK // 16, 2 * CHUNK // 16)
         pair_min = []
         recents = []
         spent = keep.tile([P, PAIRS], F32, name="spent")
@@ -174,15 +183,10 @@ def tile_list_case_link_features_kernel(
             first = ring.tile([P, PAIRS], F32, name="first", tag="first", bufs=3)
             second = ring.tile([P, PAIRS], F32, name="second", tag="second", bufs=2)
             recent = keep.tile([P, KEPT], F32, name="recent%d" % t)
-            picks = (
-                (first[:, low], pos1_sb[:, low16]),
-                (first[:, high], pos1_sb[:, high16]),
-                (second[:, low], pos2_sb[:, low16]),
-                (second[:, high], pos2_sb[:, high16]),
-            )
+            picks = (None, first[:, high], second[:, low], second[:, high])
             if t + 1 < PACK:
                 used_terms = []
-            for c, (place, offsets) in enumerate(picks):
+            for c, place in enumerate(picks):
                 if t + 1 < PACK:
                     e1, e2, e3 = products(t + 1, c)
                     if c + 1 < len(picks):
@@ -206,7 +210,9 @@ def tile_list_case_link_features_kernel(
                         ALU.add if c == 0 else ALU.subtract,
                     )
                     used_terms.append(terms)
-                nc.vector.tensor_copy(place, h[t][:].indirect(offsets))
+                if c == 1:
+                    nc.vector.tensor_copy(first[:], h[t][:].indirect(pos1_sb[:]))
+            nc.vector.tensor_copy(second[:], h[t][:].indirect(pos2_sb[:]))
             nc.vector.tensor_copy(recent[:], h[t][:].indirect(pos4_sb[:]))
             a1 = keep.tile([P, PAIRS], F32, name="a1_%d" % t, tag="a1_%d" % t)
             nc.vector.tensor_tensor(a1[:], first[:], second[:], ALU.min)

from contextlib import ExitStack

import math

import concourse.mybir as mybir

K, H, N, T, S, PAIRS, KEPT = 512, 512, 768, 4096, 2048, 1024, 512
FLOPS = 2 * K * H * S * 3 + 2 * H * N * KEPT

F32 = mybir.dt.float32
BF16 = mybir.dt.bfloat16
I32 = mybir.dt.int32
U32 = mybir.dt.uint32
U16 = mybir.dt.uint16
U8 = mybir.dt.uint8
FP8X4 = mybir.dt.float8_e4m3fn_x4
FP4X4 = mybir.dt.float4_e2m1fn_x4
ACT = mybir.ActivationFunctionType
ALU = mybir.AluOpType

P = 128
PACK = 4
CHUNK = 512
OUT_CHUNKS = (256, 128, 128)


def load_scale_rows(queue, plane, scales):
    for row in range(4):
        queue.dma_start(
            out=plane[row:P:32, :].bitcast(I32),
            in_=scales[0, row:16:4, :].bitcast(I32),
        )


def tile_list_case_link_features_kernel(
    tc, tab_words, tab_scales, w1, w2_words, w2_scales, b2, w3, w4_words, w4_scales,
    offs, pos1, pos2, pos3, pos4, out,
):
    nc = tc.nc
    with ExitStack() as ctx:
        keep = ctx.enter_context(tc.tile_pool(name="keep", bufs=1))
        ring = ctx.enter_context(tc.tile_pool(name="ring", bufs=3))
        psum = ctx.enter_context(tc.psum_pool(name="psum", bufs=1))

        offs_sb = keep.tile([P, S // 16], U16, name="offs_sb")
        pos1_sb = keep.tile([P, PAIRS // 16], U16, name="pos1_sb")
        pos2_sb = keep.tile([P, PAIRS // 16], U16, name="pos2_sb")
        pos3_sb = keep.tile([P, KEPT // 16], U16, name="pos3_sb")
        pos4_sb = keep.tile([P, KEPT // 16], U16, name="pos4_sb")

        tab_plane = keep.tile([P, T], U8, name="tab_plane", align_bytes=64)
        tab_codes = keep.tile([P, T], U32, name="tab_codes", align_bytes=64)
        w2_plane_raw = keep.tile([P, H], U8, name="w2_plane_raw", tag="plane_in", align_bytes=64)
        w2_raw = keep.tile([P, 2 * H], U8, name="w2_raw", tag="codes_in", align_bytes=64)
        w1_raw = keep.tile([P, PACK, H], F32, name="w1_raw")
        bias = keep.tile([P, PACK], F32, name="bias")

        plane_words = tab_plane[:].bitcast(I32)
        nc.vector.memset(plane_words[:, : 5 * T // 32], 0)
        nc.gpsimd.memset(plane_words[:, 5 * T // 32 :], 0)
        nc.gpsimd.memset(w2_plane_raw[:].bitcast(I32), 0)

        w3_raw = keep.tile([P, PACK, H], F32, name="w3_raw", tag="w3_raw", align_bytes=64)
        nc.sync.dma_start(offs_sb[:], offs)
        load_scale_rows(nc.sync, tab_plane, tab_scales)
        nc.sync.dma_start(out=w2_raw[:].bitcast(I32), in_=w2_words[0].bitcast(I32))
        nc.sync.dma_start(out=bias[:], in_=b2.rearrange("(p t) -> p t", t=PACK))
        nc.sync.dma_start(
            out=tab_codes[:].bitcast(I32), in_=tab_words[0].rearrange("p t i -> p (t i)").bitcast(I32)
        )
        load_scale_rows(nc.sync, w2_plane_raw, w2_scales)
        nc.sync.dma_start(out=w1_raw[:], in_=w1.rearrange("(p j) r -> p j r", j=PACK))
        nc.sync.dma_start(out=w3_raw[:], in_=w3.rearrange("(p j) r -> p j r", j=PACK))
        nc.sync.dma_start(pos1_sb[:], pos1)
        nc.sync.dma_start(pos2_sb[:], pos2)
        nc.sync.dma_start(pos4_sb[:], pos4)
        nc.sync.dma_start(pos3_sb[:], pos3)

        def deal_weight(raw, shares, name):
            grouped = keep.tile([P, PACK * H], BF16, name=name, align_bytes=64)
            dealt = grouped[:].rearrange("p (t m j) -> p m t j", t=PACK, j=PACK)
            source = raw[:].rearrange("p j (m t) -> p m t j", t=PACK)
            for copy, part, walk in shares:
                copy(out=dealt[:, part].rearrange(walk), in_=source[:, part].rearrange(walk))
            return grouped

        def quantise(grouped, name, codes_tag):
            width = grouped.shape[1] // PACK
            codes = keep.tile([P, width], U32, name=name + "_codes", tag=codes_tag, align_bytes=64)
            plane = keep.tile([P, width], U8, name=name + "_plane", align_bytes=64)
            nc.vector.quantize_mx(out=codes[:].bitcast(FP8X4), scales=plane[:], in_=grouped[:])
            return codes, plane

        v_plane = keep.tile([P, S], U8, name="v_plane", align_bytes=64)
        nc.vector.tensor_copy(v_plane[:], tab_plane[:].indirect(offs_sb[:]))
        v_codes = []
        for c in range(S // CHUNK):
            picked = keep.tile([P, CHUNK], U32, name="v_codes%d" % c, align_bytes=64)
            cols = slice(c * CHUNK // 16, (c + 1) * CHUNK // 16)
            nc.vector.tensor_copy(picked[:], tab_codes[:].indirect(offs_sb[:, cols]))
            v_codes.append(picked)

        w2_codes = keep.tile([P, 2 * H], U8, name="w2_codes", align_bytes=64)
        w2_plane = keep.tile([P, H], U8, name="w2_plane", align_bytes=64)
        nc.scalar.copy(
            out=w2_codes[:].bitcast(U16).rearrange("p (t m) -> p t m", t=PACK),
            in_=w2_raw[:].bitcast(U16).rearrange("p (m t) -> p t m", t=PACK),
        )
        nc.gpsimd.tensor_copy(
            out=w2_plane[:].rearrange("p (t m) -> p t m", t=PACK),
            in_=w2_plane_raw[:].rearrange("p (m t) -> p t m", t=PACK),
        )
        half_bias = keep.tile([P, PACK], F32, name="half_bias")
        nc.gpsimd.tensor_scalar(half_bias[:], bias[:], 0.5, 0.0, ALU.mult, ALU.add)
        one = keep.tile([P, 1], F32, name="one")
        half_pi = keep.tile([P, 1], F32, name="half_pi")
        nc.gpsimd.memset(one[:], 1.0)
        nc.gpsimd.tensor_scalar(half_pi[:], one[:], math.pi / 2, 0.0, ALU.mult, ALU.add)
        w1_grouped = deal_weight(
            w1_raw,
            (
                (nc.scalar.copy, slice(0, 40), "p m t j -> p m t j"),
                (nc.gpsimd.tensor_copy, slice(40, P), "p m t j -> p t m j"),
            ),
            "w1_grouped",
        )
        w3_grouped = deal_weight(
            w3_raw, ((nc.vector.tensor_copy, slice(0, P), "p m t j -> p m t j"),), "w3_grouped"
        )
        w1_codes, w1_plane = quantise(w1_grouped, "w1", "w3_raw")
        w3_codes, w3_plane = quantise(w3_grouped, "w3", "w3_codes")

        w4_codes = keep.tile([P, N], U32, name="w4_codes", tag="codes_in", align_bytes=64)
        w4_plane = keep.tile([P, N], U8, name="w4_plane", tag="plane_in", align_bytes=64)
        nc.gpsimd.memset(w4_plane[:].bitcast(I32), 0)
        nc.sync.dma_start(
            out=w4_codes[:].bitcast(I32),
            in_=w4_words[0].rearrange("p c i -> p (c i)").bitcast(I32),
        )
        load_scale_rows(nc.sync, w4_plane, w4_scales)

        def products(t, c):
            rows = slice(t * P, (t + 1) * P)
            cols = slice(c * CHUNK, (c + 1) * CHUNK)
            moving = v_codes[c][:].bitcast(FP8X4)
            e2 = psum.tile([P, CHUNK], F32, name="e2", tag="e2", bufs=2)
            e1 = psum.tile([P, CHUNK], F32, name="e1", tag="e1", bufs=3)
            e3 = psum.tile([P, CHUNK], F32, name="e3", tag="e3", bufs=3)
            for acc, codes, plane in (
                (e2, w2_codes[:, 2 * t * P : 2 * (t + 1) * P].bitcast(FP4X4), w2_plane),
                (e3, w3_codes[:, rows].bitcast(FP8X4), w3_plane),
                (e1, w1_codes[:, rows].bitcast(FP8X4), w1_plane),
            ):
                nc.tensor.matmul_mx(
                    out=acc[:], lhsT=codes, lhsT_scale=plane[:, rows], rhs=moving,
                    rhs_scale=v_plane[:, cols], start=True, stop=True,
                )
            return e1, e2, e3

        def cosine(t, e2, size, cos):
            nc.scalar.activation(size, e2[:], ACT.Abs, bias=bias[:, t : t + 1])
            nc.scalar.activation(cos, size, ACT.Sin, bias=half_pi[:], scale=-1.0)

        def minus_cos_times(t, e1, e2, sine, square, prod):
            nc.scalar.activation(sine, e2[:], ACT.Sin, bias=half_bias[:, t : t + 1], scale=0.5)
            nc.scalar.activation(square, sine, ACT.Square, scale=math.sqrt(2.0))
            nc.vector.scalar_tensor_tensor(prod, square, 1.0, e1[:], ALU.subtract, ALU.mult)

        h = [keep.tile([P, S], F32, name="h%d" % t) for t in range(PACK)]
        for c in range(S // CHUNK):
            e1, e2, e3 = products(0, c)
            spare = ring.tile([P, CHUNK], F32, name="cos", bufs=4)
            prod = ring.tile([P, CHUNK], F32, name="prod")
            sine, square = (spare[:], w1_raw[:, c, :]) if c == 0 else (w1_raw[:, c, :], spare[:])
            minus_cos_times(0, e1, e2, sine, square, prod[:])
            nc.vector.tensor_tensor(h[0][:, c * CHUNK : (c + 1) * CHUNK], e3[:], prod[:], ALU.subtract)

        low, high = slice(0, CHUNK), slice(CHUNK, 2 * CHUNK)
        pair_min = []
        recents = []
        spent = keep.tile([P, PAIRS], F32, name="spent")
        for t in range(PACK):
            first = ring.tile([P, PAIRS], F32, name="first", tag="first", bufs=3)
            second = ring.tile([P, PAIRS], F32, name="second", tag="second", bufs=2)
            recent = keep.tile([P, KEPT], F32, name="recent%d" % t)
            picks = (None, first[:, high], second[:, low], second[:, high])
            if t + 1 < PACK:
                used_terms = []
            for c, place in enumerate(picks):
                if t + 1 < PACK:
                    e1, e2, e3 = products(t + 1, c)
                    if c + 1 < len(picks):
                        terms = ring.tile([P, 2 * CHUNK], F32, name="terms")
                        angle = ring.tile([P, CHUNK], F32, name="angle", bufs=2)
                    else:
                        terms = keep.tile([P, 2 * CHUNK], F32, name="terms%d" % t, tag="a1_%d" % t)
                        angle = recent
                    if c == 0:
                        cos = ring.tile([P, CHUNK], F32, name="cos", bufs=4)
                        prod = spent[:, low]
                        cosine(t + 1, e2, angle[:], cos[:])
                        nc.scalar.copy(terms[:, low], e1[:])
                        nc.gpsimd.tensor_tensor(prod, terms[:, low], cos[:], ALU.mult)
                    else:
                        prod = terms[:, low]
                        minus_cos_times(t + 1, e1, e2, angle[:], place, prod)
                    nc.scalar.copy(terms[:, high], e3[:])
                    nc.gpsimd.tensor_tensor(
                        h[t + 1][:, c * CHUNK : (c + 1) * CHUNK], terms[:, high], prod,
                        ALU.add if c == 0 else ALU.subtract,
                    )
                    used_terms.append(terms)
                if c == 1:
                    nc.vector.tensor_copy(first[:], h[t][:].indirect(pos1_sb[:]))
            nc.vector.tensor_copy(second[:], h[t][:].indirect(pos2_sb[:]))
            nc.vector.tensor_copy(recent[:], h[t][:].indirect(pos4_sb[:]))
            a1 = keep.tile([P, PAIRS], F32, name="a1_%d" % t, tag="a1_%d" % t)
            nc.vector.tensor_tensor(a1[:], first[:], second[:], ALU.min)
            pair_min.append(a1)
            recents.append(recent)
            spent = first

        last_size = keep.tile([P, KEPT], F32, name="last_size")
        sizes = [terms[:, low] for terms in used_terms[: PACK - 1]] + [last_size[:]]
        for t in range(PACK):
            nc.scalar.activation(sizes[t], recents[t][:], ACT.Abs)

        m0 = 0
        out_rows = out.rearrange("(a p) m -> p a m", p=P)
        for i, width in enumerate(OUT_CHUNKS):
            last = i == len(OUT_CHUNKS) - 1
            cols = slice(m0, m0 + width)
            if last:
                place = keep.tile([P, PACK * width], F32, name="last_sums", tag="a2_grouped0", align_bytes=64)[:]
            else:
                place = (first[:], second[:, low])[i]
            a2 = place.rearrange("p (t m) -> p t m", t=PACK)
            for t in range(PACK):
                nc.vector.tensor_tensor(
                    a2[:, t, :],
                    pair_min[t][:].indirect(pos3_sb[:, m0 // 16 : (m0 + width) // 16]),
                    sizes[t][:, cols],
                    ALU.add,
                )
            grouped = keep.tile([P, PACK * width], BF16, name="a2_grouped%d" % i, tag="a2_grouped%d" % i, align_bytes=64)
            copy = nc.vector.tensor_copy if last else nc.scalar.copy
            copy(
                out=grouped[:].rearrange("p (c i t) -> p c t i", i=4, t=PACK),
                in_=a2.rearrange("p t (c i) -> p c t i", i=4),
            )
            codes = keep.tile([P, width], U32, name="a2_codes%d" % i, align_bytes=64)
            plane = keep.tile([P, width], U8, name="a2_plane%d" % i, align_bytes=64)
            nc.vector.quantize_mx(out=codes[:].bitcast(FP8X4), scales=plane[:], in_=grouped[:])
            per_bank = 2 if width == 256 else 3
            for b in range(N // P // per_bank):
                acc = psum.tile([P, per_bank, width], F32, name="acc", tag="e1" if i % 2 == 0 else "e3", bufs=3)
                for a in range(per_bank):
                    n_cols = slice((b * per_bank + a) * P, (b * per_bank + a + 1) * P)
                    nc.tensor.matmul_mx(
                        out=acc[:, a, :], lhsT=w4_codes[:, n_cols].bitcast(FP8X4),
                        lhsT_scale=w4_plane[:, n_cols], rhs=codes[:].bitcast(FP8X4),
                        rhs_scale=plane[:], start=True, stop=True,
                    )
                staged = keep.tile([P, per_bank, width], F32, name="staged%d_%d" % (i, b))
                drain = nc.vector.tensor_copy if last and b % 2 == 1 else nc.scalar.copy
                drain(out=staged[:], in_=acc[:])
                nc.sync.dma_start(
                    out=out_rows[:, b * per_bank : (b + 1) * per_bank, cols], in_=staged[:]
                )
            m0 = m0 + width
